import numpy as np, ml_dtypes
CORES = [0,1,2,3]
N = 4
def setup_inputs(rng):
    return {"x": rng.standard_normal((N, 128 // N, 16), dtype=np.float32).astype(ml_dtypes.bfloat16)}
def reference(x):
    g = np.concatenate(list(x), axis=0)
    return {"y": np.broadcast_to(g, (N,) + g.shape)}

from concourse.bass import DstId, RemoteDMATransfer

N = 4
ENGINES = 0x0001
NENG = 1

SCRATCH = {
    "land": ("dram", [N, 128, 4], "bfloat16"),
}
SEMAPHORES = ["loaded", "moved", "stored"]


def rank_program(g, core, T, topo):
    rank = T.rank_of(core)
    if rank is None:
        return

    g.sync.dma_start(T.land[rank], T.x[:]).then_inc(T.sem.loaded, 16)
    g.wait_ge(T.sem.loaded, 16)

    peers = [c for c in T.cores if c != core]
    ids = []
    for c in peers:
        rid, pid, _se = topo.addr(c)
        ids.append(DstId(rid=rid, pnc=pid))
    g.remote_dma_fused(
        [RemoteDMATransfer(dst_ids=ids, dma_engine_mask=ENGINES, remote_sem=T.sem.moved,
                           srcs=[T.land[rank]], dsts=[T.land[rank] for _c in peers])],
        local_sem=T.sem.moved)

    g.wait_ge(T.sem.moved, NENG * N)

    g.sync.wait_ge(T.sem.moved, NENG * N)
    g.sync.dma_start(T.y[:], T.land[:]).then_inc(T.sem.stored, 16)
    g.sync.wait_ge(T.sem.stored, 16)
